import numpy as np
import ml_dtypes


def mxq(x, axis, fmt="e4m3"):
    dtype, down = {"e4m3": (ml_dtypes.float8_e4m3fn, 7), "e5m2": (ml_dtypes.float8_e5m2, 14)}[fmt]
    v = np.moveaxis(np.asarray(x, np.float32).astype(ml_dtypes.bfloat16).astype(np.float64), axis, -1)
    blocks = v.reshape(v.shape[:-1] + (-1, 32))
    amax = np.abs(blocks).max(-1, keepdims=True)
    byte = np.maximum(np.where(amax > 0, np.frexp(amax)[1] - 1 + 127, 0) - down, 1)
    scale = np.exp2(byte - 127.0)
    codes = (blocks / scale).astype(np.float32).astype(dtype).astype(np.float64)
    return np.moveaxis((codes * scale).reshape(v.shape), -1, axis)


WIDE = False


def mx_kscale(k):
    if not WIDE:
        return np.ones(k)
    levels = np.array([10, -10, 5, -5, 0])
    if k % 512:
        return np.exp2(np.random.permutation(np.resize(levels, k // 32))).repeat(32)
    a = np.empty((k // 512, 16))
    for p in range(k // 512):
        a[p, :8] = np.random.permutation(np.resize(levels, 8))
        for g in range(8):
            far = levels[np.abs(levels - a[p, g]) >= 10]
            a[p, g + 8] = far[np.random.randint(len(far))]
    return np.exp2(a.ravel()).repeat(32)


def f64(x):
    return np.asarray(x).astype(np.float64)


def striped(idx):
    return np.tile(idx.reshape(-1, 16).T, (8, 1)).astype(np.uint16)


def unstriped(offs):
    return offs[:16].T.reshape(-1).astype(np.int64)


E2M1 = np.array([0.0, 0.5, 1.0, 1.5, 2.0, 3.0, 4.0, 6.0, -0.0, -0.5, -1.0, -1.5, -2.0, -3.0, -4.0, -6.0])


def pack_weight(w, fmt):
    k, n = w.shape
    w = f64(np.asarray(w, np.float32).astype(ml_dtypes.bfloat16)).reshape(k // 32, 32, n)
    amax = np.abs(w).max(1)
    if fmt == "e4m3":
        byte = np.frexp(amax)[1] - 1 + 127 - 7
    else:
        mant, ex = np.frexp(amax / 6.0)
        byte = np.where(mant > 0.5, ex, ex - 1) + 127
    byte = np.clip(np.where(amax > 0, byte, 1), 1, 254)
    scaled = (w * np.exp2(127.0 - byte)[:, None, :]).reshape(k, n).astype(np.float32)
    by_word = np.ascontiguousarray(scaled.reshape(k // 512, 128, 4, n).transpose(0, 1, 3, 2))
    if fmt == "e4m3":
        words = by_word.astype(ml_dtypes.float8_e4m3fn).view(np.uint8)
    else:
        c = by_word.astype(ml_dtypes.float4_e2m1fn).view(np.uint8) & 0xF
        words = (c[..., 0::2] | (c[..., 1::2] << 4)).reshape(k // 512, 128, 2 * n)
    return np.ascontiguousarray(words), np.ascontiguousarray(byte.astype(np.uint8).reshape(k // 512, 16, n))


def unpack_weight(words, scales, fmt):
    g, _, n = scales.shape
    words = np.ascontiguousarray(words).reshape(g, 128, n, -1)
    if fmt == "e4m3":
        vals = words.view(ml_dtypes.float8_e4m3fn).astype(np.float64)
    else:
        nib = np.empty((g, 128, n, 4), np.uint8)
        nib[..., 0::2] = words & 0xF
        nib[..., 1::2] = words >> 4
        vals = E2M1[nib]
    vals = vals * np.repeat(np.exp2(scales.astype(np.float64) - 127.0), 8, axis=1)[..., None]
    return vals.transpose(0, 1, 3, 2).reshape(g * 512, n)


def gelu(v):
    return 0.5 * v * (1.0 + np.tanh(np.sqrt(2.0 / np.pi) * (v + 0.044715 * v**3)))


K, H, T, S, T2, P = 1024, 1024, 2048, 512, 1024, 512


def setup_inputs():
    n = np.random.standard_normal
    s = mx_kscale(K)[:, None]
    u = mx_kscale(H)[:, None]
    tab_words, tab_scales = pack_weight(n((K, T)) * s, "e4m3")
    w4_words, w4_scales = pack_weight(n((K, H)) * 0.56 / np.sqrt(K) / s, "e2m1")
    return {
        "tab_words": tab_words, "tab_scales": tab_scales,
        "w1": (n((K, H)) * 0.8 / np.sqrt(K) / s * u.T).astype(np.float32),
        "w4_words": w4_words, "w4_scales": w4_scales,
        "base": (n((H, S)) * 0.8 * u).astype(np.float32),
        "wgs": np.exp(0.3 * n((128, S))).astype(np.float32),
        "page0": (n((H, T2)) * u).astype(np.float32),
        "low": ((0.5 * n(H) - 0.3) * u[:, 0]).astype(np.float32),
        "shift": (0.7 * n(H) * u[:, 0]).astype(np.float32),
        "gain": (1.8 * n(H) / np.sqrt(H) / u[:, 0] ** 2).astype(np.float32),
        "pw": np.exp(0.4 * n(P)).astype(np.float32),
        "offs": striped(np.random.permutation(T)[:S]),
        "offs2": striped(np.random.permutation(T2)[:S]),
        "offs3": striped(np.random.permutation(T2)[:P]),
        "offs4": striped(np.random.permutation(T2)[:P]),
    }


def reference(tab_words, tab_scales, w1, w4_words, w4_scales, base, wgs, page0, low, shift, gain, pw,
              offs, offs2, offs3, offs4):
    v = unpack_weight(tab_words, tab_scales, "e4m3")[:, unstriped(offs)]
    w4 = unpack_weight(w4_words, w4_scales, "e2m1")
    lin = (mxq(f64(w1), 0, "e4m3").T @ v) + f64(base)
    h = lin * np.cos(w4.T @ v)
    page = f64(page0).copy()
    page[:, unstriped(offs2)] = np.tile(f64(wgs), (H // 128, 1)) * h
    x1 = np.maximum(page[:, unstriped(offs3)], f64(low)[:, None])
    x2 = (page[:, unstriped(offs4)] + f64(shift)[:, None]) * f64(gain)[:, None]
    e = mxq(x1, 0, "e4m3").T @ mxq(x2, 0, "e4m3")
    return f64(pw)[:, None] / (1.0 + np.exp(-e))

@@ -1,0 +1,321 @@
+import math
+from contextlib import ExitStack
+
+import concourse.mybir as mybir
+
+K, H, T, S, T2, P = 1024, 1024, 2048, 512, 1024, 512
+FLOPS = 2 * K * H * S * 2 + 2 * H * P * P
+
+F32 = mybir.dt.float32
+BF16 = mybir.dt.bfloat16
+I32 = mybir.dt.int32
+U32 = mybir.dt.uint32
+U16 = mybir.dt.uint16
+U8 = mybir.dt.uint8
+FP8X4 = mybir.dt.float8_e4m3fn_x4
+FP4X4 = mybir.dt.float4_e2m1fn_x4
+ALU = mybir.AluOpType
+ACT = mybir.ActivationFunctionType
+
+PART = 128
+PACK = 4
+PASS = PART * PACK
+QUAD = 32
+SLICES = H // PART
+F32_MAX = 3.4028234663852886e38
+USE_POOL = True
+
+
+def tile_list_powder_chip_binning_kernel(
+    tc, tab_words, tab_scales, w1, w4_words, w4_scales, base, wgs, page0, low, shift, gain, pw,
+    offs, offs2, offs3, offs4, out,
+):
+    nc = tc.nc
+    with ExitStack() as ctx:
+        sb = ctx.enter_context(tc.tile_pool(name="sb", bufs=1))
+        ps = ctx.enter_context(tc.psum_pool(name="ps", bufs=1))
+
+        def alloc(name, shape, dtype, tag=None):
+            return sb.tile(shape, dtype, name=name, tag=tag or name, align_bytes=64)
+
+        lists = [alloc(f"list{i}", [PART, S // 16], U16) for i in range(4)]
+        tab_w = [alloc(f"tab_w{a}", [PART, T], U32) for a in range(2)]
+        tab_s = alloc("tab_s", [PART, 2, T], U8)
+        w4_w = alloc("w4_w", [PART, 2, 2 * H], U8)
+        w4_s = alloc("w4_s", [PART, 2, H], U8)
+        w1_raw = [[alloc(f"w1_raw{s}_{a}", [PART, PACK, PART], F32) for a in range(2)] for s in range(PACK)]
+        w1_raw_hi = [alloc(f"w1_raw_hi{a}", [PART, PACK, PASS], F32) for a in range(2)]
+        rows = [alloc(f"rows{s}", [PART, S], F32) for s in range(SLICES)]
+        pages = [alloc(f"page{s}", [PART, T2], F32) for s in range(SLICES)]
+        wgs_lo = alloc("wgs_lo", [PART, S], F32)
+        wgs_hi = alloc("wgs_hi", [PART, PACK, S], F32)
+        vec = {}
+        for name in ("low", "shift", "gain"):
+            for b in range(2):
+                vec[name, b] = alloc(f"{name}{b}", [PART, PACK], F32)
+        pw_sb = alloc("pw_sb", [PART, PACK], F32)
+
+        def slice_rows(mat, s):
+            if s < PACK:
+                return mat[s * PART : (s + 1) * PART, :]
+            return mat[PASS:, :].rearrange("(p t) c -> p t c", t=PACK)[:, s - PACK, :]
+
+        def load_w1_lo(s):
+            for a in range(2):
+                src = w1[a * PASS : (a + 1) * PASS, s * PART : (s + 1) * PART]
+                nc.sync.dma_start(out=w1_raw[s][a][:], in_=src.rearrange("(p j) c -> p j c", j=PACK))
+
+        def load_base(s):
+            nc.sync.dma_start(out=rows[s][:], in_=slice_rows(base, s))
+
+        def load_page(s):
+            nc.sync.dma_start(out=pages[s][:], in_=slice_rows(page0, s))
+
+        nc.vector.memset(tab_s[:].rearrange("p a n -> p (a n)").bitcast(I32), 0)
+        nc.vector.memset(w4_s[:].rearrange("p a n -> p (a n)").bitcast(I32), 0)
+        for q in range(4):
+            nc.gpsimd.dma_start(
+                out=tab_s[QUAD * q : QUAD * q + 4, :, :].bitcast(I32),
+                in_=tab_scales[:, 4 * q : 4 * q + 4, :].rearrange("a r n -> r a n").bitcast(I32),
+            )
+        for q in range(4):
+            nc.scalar.dma_start(
+                out=w4_s[QUAD * q : QUAD * q + 4, :, :].bitcast(I32),
+                in_=w4_scales[:, 4 * q : 4 * q + 4, :].rearrange("a r n -> r a n").bitcast(I32),
+            )
+
+        nc.sync.dma_start(lists[0][:], offs)
+        for a in range(2):
+            nc.sync.dma_start(
+                out=tab_w[a][:].bitcast(I32), in_=tab_words[a].rearrange("p n t -> p (n t)").bitcast(I32)
+            )
+        nc.sync.dma_start(out=w4_w[:].bitcast(I32), in_=w4_words.rearrange("a p c -> p a c").bitcast(I32))
+        load_w1_lo(0)
+        load_base(0)
+        nc.sync.dma_start(out=wgs_lo[:], in_=wgs)
+        load_w1_lo(1)
+        nc.sync.dma_start(lists[1][:], offs2)
+        load_page(0)
+        load_base(1)
+        nc.sync.dma_start(lists[3][:], offs4)
+        nc.sync.dma_start(lists[2][:], offs3)
+        load_w1_lo(2)
+        load_page(1)
+        load_base(2)
+        load_w1_lo(3)
+        load_base(3)
+        for a in range(2):
+            src = w1[a * PASS : (a + 1) * PASS, PASS:]
+            nc.sync.dma_start(out=w1_raw_hi[a][:], in_=src.rearrange("(p j) c -> p j c", j=PACK))
+        load_page(2)
+        with nc.allow_non_contiguous_dma(reason="one value to a partition"):
+            for name, src in (("low", low), ("shift", shift), ("gain", gain)):
+                nc.sync.dma_start(out=vec[name, 0][:], in_=src[:PASS].rearrange("(s p) -> p s", p=PART))
+                nc.sync.dma_start(out=vec[name, 1][:], in_=src[PASS:].rearrange("(p t) -> p t", t=PACK))
+            nc.sync.dma_start(out=pw_sb[:], in_=pw.rearrange("(c p) -> p c", p=PART))
+        load_page(3)
+        load_base(4)
+        for q in range(4):
+            nc.sync.dma_start(
+                out=wgs_hi[QUAD * q : QUAD * (q + 1), :, :], in_=wgs.rearrange("(p t) j -> p t j", t=PACK)
+            )
+        for s in range(PACK + 1, SLICES):
+            load_base(s)
+        for s in range(PACK, SLICES):
+            load_page(s)
+
+        v_w = [alloc(f"v_w{a}", [PART, S], U32) for a in range(2)]
+        v_s = [alloc(f"v_s{a}", [PART, S], U8) for a in range(2)]
+        for a in range(2):
+            nc.vector.tensor_copy(v_s[a][:], tab_s[:, a, :].indirect(lists[0][:]))
+        for a in range(2):
+            nc.vector.tensor_copy(v_w[a][:], tab_w[a][:].indirect(lists[0][:]))
+
+        w4_wd = alloc("w4_wd", [PART, 2, PACK, 2 * PART], U8)
+        w4_sd = alloc("w4_sd", [PART, 2, PACK, PART], U8)
+        nc.vector.tensor_copy(
+            out=w4_wd[:].bitcast(U16),
+            in_=w4_w[:].bitcast(U16)[:, :, PASS:].rearrange("p a (m t) -> p a t m", t=PACK),
+        )
+        nc.vector.tensor_copy(out=w4_sd[:], in_=w4_s[:, :, PASS:].rearrange("p a (m t) -> p a t m", t=PACK))
+
+        w1_c = {}
+        w1_s = {}
+
+        def quantise_w1_lo(s):
+            grouped = alloc(f"w1_g{s}", [PART, 2, PART, PACK], BF16)
+            for a in range(2):
+                nc.scalar.copy(
+                    out=grouped[:, a].rearrange("p (c i) j -> p c j i", i=4),
+                    in_=w1_raw[s][a][:].rearrange("p j (c i) -> p c j i", i=4),
+                )
+            codes = alloc(f"w1_c{s}", [PART, 2 * PART], U32)
+            scales = alloc(f"w1_s{s}", [PART, 2 * PART], U8)
+            nc.vector.quantize_mx(
+                out=codes[:].bitcast(FP8X4), scales=scales[:], in_=grouped[:].rearrange("p a c j -> p (a c j)")
+            )
+            for a in range(2):
+                w1_c[s, a] = codes[:, a * PART : (a + 1) * PART]
+                w1_s[s, a] = scales[:, a * PART : (a + 1) * PART]
+
+        def quantise_w1_hi():
+            for a in range(2):
+                grouped = alloc(f"w1_gh{a}", [PART, PACK, PART, PACK], BF16)
+                nc.scalar.copy(
+                    out=grouped[:].rearrange("p t m j -> p m j t"),
+                    in_=w1_raw_hi[a][:].rearrange("p j (m t) -> p m j t", t=PACK),
+                )
+                codes = alloc(f"w1_ch{a}", [PART, PASS], U32)
+                scales = alloc(f"w1_sh{a}", [PART, PASS], U8)
+                nc.vector.quantize_mx(
+                    out=codes[:].bitcast(FP8X4), scales=scales[:], in_=grouped[:].rearrange("p t m j -> p (t m j)")
+                )
+                for t in range(PACK):
+                    w1_c[PACK + t, a] = codes[:, t * PART : (t + 1) * PART]
+                    w1_s[PACK + t, a] = scales[:, t * PART : (t + 1) * PART]
+
+        def w4_operand(s, a):
+            if s < PACK:
+                return w4_w[:, a, 2 * PART * s : 2 * PART * (s + 1)], w4_s[:, a, PART * s : PART * (s + 1)]
+            return w4_wd[:, a, s - PACK, :], w4_sd[:, a, s - PACK, :]
+
+        put_tags = ["w1_g1", "put1", "put2", "put3", "w1_g0", "put5", "put6", "put7"]
+        g1_tags = ["g1_0", "g1_1", "w1_gh1"]
+        g2_tags = ["w1_g2", "w1_g3", "w1_gh0"]
+        put = {}
+
+        def stage_one(s):
+            arg = ps.tile([PART, S], F32, name=f"arg{s}", tag=f"arg{s % 2}")
+            lin = ps.tile([PART, S], F32, name=f"lin{s}", tag=f"lin{s % 2}")
+            for a in range(2):
+                words, scales = w4_operand(s, a)
+                nc.tensor.matmul_mx(
+                    out=arg[:], lhsT=words.bitcast(FP4X4), lhsT_scale=scales,
+                    rhs=v_w[a][:].bitcast(FP8X4), rhs_scale=v_s[a][:], start=(a == 0), stop=(a == 1),
+                )
+            for a in range(2):
+                nc.tensor.matmul_mx(
+                    out=lin[:], lhsT=w1_c[s, a].bitcast(FP8X4), lhsT_scale=w1_s[s, a],
+                    rhs=v_w[a][:].bitcast(FP8X4), rhs_scale=v_s[a][:], start=(a == 0), stop=(a == 1),
+                )
+            mag = alloc(f"mag{s}", [PART, S], F32, tag=f"mag{s % 2}")
+            cos = alloc(f"cos{s}", [PART, S], F32, tag=f"cos{s % 3}")
+            nc.scalar.activation(mag[:], arg[:], ACT.Abs)
+            nc.scalar.activation(cos[:], mag[:], ACT.Sin, bias=math.pi / 2, scale=-1.0)
+            weight = wgs_lo[:] if s < PACK else wgs_hi[:, s - PACK, :]
+            h = rows[s]
+            if not USE_POOL:
+                put[s] = alloc(f"put{s}", [PART, S], F32, tag=put_tags[s])
+                nc.vector.tensor_tensor(h[:], lin[:], h[:], ALU.add)
+                nc.vector.tensor_tensor(put[s][:], h[:], cos[:], ALU.mult)
+                return
+            if s == 0:
+                eng = nc.vector
+                eng.tensor_tensor(h[:], lin[:], h[:], ALU.add)
+            else:
+                eng = nc.gpsimd
+                lin_sb = alloc(f"lin_sb{s}", [PART, S], F32, tag=f"lin_sb{s % 3}")
+                nc.scalar.copy(out=lin_sb[:], in_=lin[:])
+                eng.tensor_tensor(h[:], lin_sb[:], h[:], ALU.add)
+            eng.tensor_tensor(h[:], h[:], cos[:], ALU.mult)
+            put[s] = alloc(f"put{s}", [PART, S], F32, tag=put_tags[s])
+            eng.tensor_tensor(put[s][:], h[:], weight, ALU.mult)
+
+        picked = {}
+
+        def look_up(s):
+            if USE_POOL:
+                nc.vector.tensor_copy(pages[s][:].indirect(lists[1][:]), put[s][:])
+            else:
+                weight = wgs_lo[:] if s < PACK else wgs_hi[:, s - PACK, :]
+                nc.vector.tensor_tensor(pages[s][:].indirect(lists[1][:]), put[s][:], weight, ALU.mult)
+            g1 = alloc(f"g1_{s}", [PART, P], F32, tag=g1_tags[s % 3] if s < SLICES - 1 else "lin_sb1")
+            g2 = alloc(f"g2_{s}", [PART, P], F32, tag=g2_tags[s % 3] if s < SLICES - 1 else "mag1")
+            nc.vector.tensor_copy(g2[:], pages[s][:].indirect(lists[3][:]))
+            nc.vector.tensor_copy(g1[:], pages[s][:].indirect(lists[2][:]))
+            picked[s] = (g1, g2)
+
+        bias2 = [alloc(f"bias2_{b}", [PART, PACK], F32) for b in range(2)]
+        half_pw = alloc("half_pw", [PART, PACK], F32)
+
+        def finish(s, x1_out, x2_out):
+            b, t = divmod(s, PACK)
+            g1, g2 = picked[s]
+            eng = nc.gpsimd if USE_POOL else nc.vector
+            eng.tensor_scalar(x1_out, g1[:], F32_MAX, vec["low", b][:, t : t + 1], ALU.min, ALU.max)
+            nc.scalar.activation(
+                x2_out, g2[:], ACT.Identity, bias=bias2[b][:, t : t + 1], scale=vec["gain", b][:, t : t + 1]
+            )
+
+        def quantise_x(name, grouped, tag):
+            codes = alloc(f"{name}_c", [PART, P], U32, tag=tag)
+            scales = alloc(f"{name}_s", [PART, P], U8)
+            nc.vector.quantize_mx(
+                out=codes[:].bitcast(FP8X4), scales=scales[:], in_=grouped[:].rearrange("p m t -> p (m t)")
+            )
+            return codes, scales
+
+        e = [ps.tile([PART, P], F32, name=f"e{c}") for c in range(PACK)]
+
+        def match(x1, x2, b):
+            for c in range(PACK):
+                cols = slice(c * PART, (c + 1) * PART)
+                nc.tensor.matmul_mx(
+                    out=e[c][:], lhsT=x1[0][:, cols].bitcast(FP8X4), lhsT_scale=x1[1][:, cols],
+                    rhs=x2[0][:].bitcast(FP8X4), rhs_scale=x2[1][:], start=(b == 0), stop=(b == 1),
+                )
+
+        for b in range(2):
+            nc.gpsimd.tensor_tensor(bias2[b][:], vec["shift", b][:], vec["gain", b][:], ALU.mult)
+        nc.gpsimd.tensor_scalar(half_pw[:], pw_sb[:], 0.5, 0.0, ALU.mult, ALU.add)
+
+        planes = None
+        flats = {}
+        quantise_w1_lo(0)
+        quantise_w1_lo(1)
+        for s in range(SLICES):
+            stage_one(s)
+            if s + 2 < PACK:
+                quantise_w1_lo(s + 2)
+            if s + 2 == PACK:
+                quantise_w1_hi()
+                planes = alloc("planes", [PART, PACK, 2, P], BF16, tag="w1_raw_hi0")
+            if 2 <= s < PACK + 2:
+                r = s - 2
+                flat = alloc(f"flat{r}", [PART, 2, P], BF16, tag=f"rows{s}")
+                finish(r, flat[:, 0, :], flat[:, 1, :])
+                flats[r] = flat
+            if 3 <= s < PACK + 3:
+                r = s - 3
+                for t in range(PACK):
+                    nc.sync.dma_start(out=planes[QUAD * r : QUAD * (r + 1), t, :, :], in_=flats[r][t:PART:PACK, :, :])
+            if s < SLICES - 1:
+                look_up(s)
+
+        lo = []
+        for i, (tag, ctag) in enumerate((("mag1", "put5"), ("lin_sb1", "put6"))):
+            grouped = alloc(f"x_lo{i}", [PART, P, PACK], BF16, tag=tag)
+            nc.scalar.copy(
+                out=grouped[:].rearrange("p (c i) t -> p c t i", i=4),
+                in_=planes[:, :, i, :].rearrange("p t (c i) -> p c t i", i=4),
+            )
+            lo.append(quantise_x(f"x_lo{i}", grouped, ctag))
+        match(lo[0], lo[1], 0)
+
+        x1_hi = alloc("x1_hi", [PART, P, PACK], BF16, tag="rows7")
+        x2_hi = alloc("x2_hi", [PART, P, PACK], BF16, tag="w1_raw_hi0")
+        for s in range(PACK, SLICES - 1):
+            finish(s, x1_hi[:, :, s - PACK], x2_hi[:, :, s - PACK])
+
+        look_up(SLICES - 1)
+        finish(SLICES - 1, x1_hi[:, :, PACK - 1], x2_hi[:, :, PACK - 1])
+        x2q = quantise_x("x2_hi", x2_hi, "x2_hi_c")
+        x1q = quantise_x("x1_hi", x1_hi, "x1_hi_c")
+        match(x1q, x2q, 1)
+
+        for c in range(PACK):
+            res = alloc(f"res{c}", [PART, P], F32, tag=f"put{c + 1}" if c < 3 else "put7")
+            nc.scalar.activation(res[:], e[c][:], ACT.Tanh, scale=0.5)
+            col = half_pw[:, c : c + 1]
+            nc.vector.tensor_scalar(res[:], res[:], col, col, ALU.mult, ALU.add)
+            nc.sync.dma_start(out=out[c * PART : (c + 1) * PART, :], in_=res[:])

@@ -42,8 +42,11 @@ def tile_list_powder_chip_binning_kernel(
         tab_w = [alloc(f"tab_w{a}", [PART, T], U32) for a in range(2)]
         tab_s = alloc("tab_s", [PART, 2, T], U8)
         w4_w = alloc("w4_w", [PART, 2, 2 * H], U8)
-        w4_s = alloc("w4_s", [PART, 2, H], U8)
-        w1_raw = [[alloc(f"w1_raw{s}_{a}", [PART, PACK, PART], F32) for a in range(2)] for s in range(PACK)]
+        w4_s = [alloc(f"w4_s{b}", [PART, 2, PASS], U8) for b in range(2)]
+        groups = {0: 1, 1: 1, 2: 2}
+        w1_raw = {
+            s: [alloc(f"w1_raw{s}_{a}", [PART, PACK, n * PART], F32) for a in range(2)] for s, n in ((0, 1), (1, 1), (2, 2))
+        }
         w1_raw_hi = [alloc(f"w1_raw_hi{a}", [PART, PACK, PASS], F32) for a in range(2)]
         rows = [alloc(f"rows{s}", [PART, S], F32) for s in range(SLICES)]
         pages = [alloc(f"page{s}", [PART, T2], F32) for s in range(SLICES)]
@@ -62,7 +65,7 @@ def tile_list_powder_chip_binning_kernel(
 
         def load_w1_lo(s):
             for a in range(2):
-                src = w1[a * PASS : (a + 1) * PASS, s * PART : (s + 1) * PART]
+                src = w1[a * PASS : (a + 1) * PASS, s * PART : (s + groups[s]) * PART]
                 nc.sync.dma_start(out=w1_raw[s][a][:], in_=src.rearrange("(p j) c -> p j c", j=PACK))
 
         def load_base(s):
@@ -71,29 +74,37 @@ def tile_list_powder_chip_binning_kernel(
         def load_page(s):
             nc.sync.dma_start(out=pages[s][:], in_=slice_rows(page0, s))
 
+        warm = alloc("warm", [PART, 2], F32)
+        nc.vector.memset(warm[:, 0:1], 0.0)
+        nc.scalar.activation(warm[:, 1:2], warm[:, 0:1], ACT.Silu)
         nc.vector.memset(tab_s[:].rearrange("p a n -> p (a n)").bitcast(I32), 0)
-        nc.vector.memset(w4_s[:].rearrange("p a n -> p (a n)").bitcast(I32), 0)
-        for q in range(4):
-            nc.gpsimd.dma_start(
-                out=tab_s[QUAD * q : QUAD * q + 4, :, :].bitcast(I32),
-                in_=tab_scales[:, 4 * q : 4 * q + 4, :].rearrange("a r n -> r a n").bitcast(I32),
-            )
-        for q in range(4):
-            nc.scalar.dma_start(
-                out=w4_s[QUAD * q : QUAD * q + 4, :, :].bitcast(I32),
-                in_=w4_scales[:, 4 * q : 4 * q + 4, :].rearrange("a r n -> r a n").bitcast(I32),
-            )
+        nc.vector.memset(w4_s[1][:].rearrange("p a n -> p (a n)").bitcast(I32), 0)
+        for b, queue in ((0, nc.scalar), (1, nc.gpsimd)):
+            for q in range(4):
+                src = w4_scales[:, 4 * q : 4 * q + 4, b * PASS : (b + 1) * PASS]
+                queue.dma_start(
+                    out=w4_s[b][QUAD * q : QUAD * q + 4, :, :].bitcast(I32),
+                    in_=src.rearrange("a r n -> r a n").bitcast(I32),
+                )
 
-        nc.sync.dma_start(lists[0][:], offs)
-        for a in range(2):
+        def load_table(a):
             nc.sync.dma_start(
                 out=tab_w[a][:].bitcast(I32), in_=tab_words[a].rearrange("p n t -> p (n t)").bitcast(I32)
             )
+
+        nc.sync.dma_start(lists[0][:], offs)
         nc.sync.dma_start(out=w4_w[:].bitcast(I32), in_=w4_words.rearrange("a p c -> p a c").bitcast(I32))
+        for q in range(4):
+            nc.sync.dma_start(
+                out=tab_s[QUAD * q : QUAD * q + 4, :, :].bitcast(I32),
+                in_=tab_scales[:, 4 * q : 4 * q + 4, :].rearrange("a r n -> r a n").bitcast(I32),
+            )
+        load_table(0)
         load_w1_lo(0)
+        load_table(1)
+        load_w1_lo(1)
         load_base(0)
         nc.sync.dma_start(out=wgs_lo[:], in_=wgs)
-        load_w1_lo(1)
         nc.sync.dma_start(lists[1][:], offs2)
         load_page(0)
         load_base(1)
@@ -102,7 +113,6 @@ def tile_list_powder_chip_binning_kernel(
         load_w1_lo(2)
         load_page(1)
         load_base(2)
-        load_w1_lo(3)
         load_base(3)
         for a in range(2):
             src = w1[a * PASS : (a + 1) * PASS, PASS:]
@@ -125,11 +135,11 @@ def tile_list_powder_chip_binning_kernel(
             load_page(s)
 
         v_w = [alloc(f"v_w{a}", [PART, S], U32) for a in range(2)]
-        v_s = [alloc(f"v_s{a}", [PART, S], U8) for a in range(2)]
-        for a in range(2):
-            nc.vector.tensor_copy(v_s[a][:], tab_s[:, a, :].indirect(lists[0][:]))
         for a in range(2):
             nc.vector.tensor_copy(v_w[a][:], tab_w[a][:].indirect(lists[0][:]))
+        v_s = alloc("v_s", [PART, 2, S], U8)
+        for a in range(2):
+            nc.vector.tensor_copy(v_s[:, a, :], tab_s[:, a, :].indirect(lists[0][:]))
 
         w4_wd = alloc("w4_wd", [PART, 2, PACK, 2 * PART], U8)
         w4_sd = alloc("w4_sd", [PART, 2, PACK, PART], U8)
@@ -137,51 +147,58 @@ def tile_list_powder_chip_binning_kernel(
             out=w4_wd[:].bitcast(U16),
             in_=w4_w[:].bitcast(U16)[:, :, PASS:].rearrange("p a (m t) -> p a t m", t=PACK),
         )
-        nc.vector.tensor_copy(out=w4_sd[:], in_=w4_s[:, :, PASS:].rearrange("p a (m t) -> p a t m", t=PACK))
+        nc.gpsimd.tensor_copy(out=w4_sd[:], in_=w4_s[1][:].rearrange("p a (m t) -> p a t m", t=PACK))
 
         w1_c = {}
         w1_s = {}
 
         def quantise_w1_lo(s):
-            grouped = alloc(f"w1_g{s}", [PART, 2, PART, PACK], BF16)
+            width = groups[s] * PART
+            grouped = alloc(f"w1_g{s}", [PART, 2, width, PACK], BF16)
             for a in range(2):
-                nc.scalar.copy(
+                copy = nc.vector.tensor_copy if s == 1 else nc.scalar.copy
+                copy(
                     out=grouped[:, a].rearrange("p (c i) j -> p c j i", i=4),
                     in_=w1_raw[s][a][:].rearrange("p j (c i) -> p c j i", i=4),
                 )
-            codes = alloc(f"w1_c{s}", [PART, 2 * PART], U32)
-            scales = alloc(f"w1_s{s}", [PART, 2 * PART], U8)
+            codes = alloc(f"w1_c{s}", [PART, 2 * width], U32)
+            scales = alloc(f"w1_s{s}", [PART, 2 * width], U8)
             nc.vector.quantize_mx(
                 out=codes[:].bitcast(FP8X4), scales=scales[:], in_=grouped[:].rearrange("p a c j -> p (a c j)")
             )
             for a in range(2):
-                w1_c[s, a] = codes[:, a * PART : (a + 1) * PART]
-                w1_s[s, a] = scales[:, a * PART : (a + 1) * PART]
+                for u in range(groups[s]):
+                    cols = slice(a * width + u * PART, a * width + (u + 1) * PART)
+                    w1_c[s + u, a] = codes[:, cols]
+                    w1_s[s + u, a] = scales[:, cols]
 
         def quantise_w1_hi():
+            grouped = alloc("w1_gh", [PART, 2, PACK, PART, PACK], BF16, tag="w1_raw2_1")
             for a in range(2):
-                grouped = alloc(f"w1_gh{a}", [PART, PACK, PART, PACK], BF16)
                 nc.scalar.copy(
-                    out=grouped[:].rearrange("p t m j -> p m j t"),
+                    out=grouped[:, a].rearrange("p t m j -> p m j t"),
                     in_=w1_raw_hi[a][:].rearrange("p j (m t) -> p m j t", t=PACK),
                 )
-                codes = alloc(f"w1_ch{a}", [PART, PASS], U32)
-                scales = alloc(f"w1_sh{a}", [PART, PASS], U8)
-                nc.vector.quantize_mx(
-                    out=codes[:].bitcast(FP8X4), scales=scales[:], in_=grouped[:].rearrange("p t m j -> p (t m j)")
-                )
+            codes = alloc("w1_ch", [PART, 2 * PASS], U32)
+            scales = alloc("w1_sh", [PART, 2 * PASS], U8)
+            nc.vector.quantize_mx(
+                out=codes[:].bitcast(FP8X4), scales=scales[:], in_=grouped[:].rearrange("p a t m j -> p (a t m j)")
+            )
+            for a in range(2):
                 for t in range(PACK):
-                    w1_c[PACK + t, a] = codes[:, t * PART : (t + 1) * PART]
-                    w1_s[PACK + t, a] = scales[:, t * PART : (t + 1) * PART]
+                    cols = slice(a * PASS + t * PART, a * PASS + (t + 1) * PART)
+                    w1_c[PACK + t, a] = codes[:, cols]
+                    w1_s[PACK + t, a] = scales[:, cols]
 
         def w4_operand(s, a):
             if s < PACK:
-                return w4_w[:, a, 2 * PART * s : 2 * PART * (s + 1)], w4_s[:, a, PART * s : PART * (s + 1)]
+                return w4_w[:, a, 2 * PART * s : 2 * PART * (s + 1)], w4_s[0][:, a, PART * s : PART * (s + 1)]
             return w4_wd[:, a, s - PACK, :], w4_sd[:, a, s - PACK, :]
 
         put_tags = ["w1_g1", "put1", "put2", "put3", "w1_g0", "put5", "put6", "put7"]
-        g1_tags = ["g1_0", "g1_1", "w1_gh1"]
-        g2_tags = ["w1_g2", "w1_g3", "w1_gh0"]
+        g1_tags = ["w1_g2", "g1_1", "g1_2"]
+        g2_tags = ["g2_0", "g2_1", "w1_raw2_1"]
+        mag_tags = ["mag0", "w1_g2", "mag0", "mag1", "w1_raw_hi1", "w1_raw_hi1", "mag0", "mag1"]
         put = {}
 
         def stage_one(s):
@@ -191,14 +208,14 @@ def tile_list_powder_chip_binning_kernel(
                 words, scales = w4_operand(s, a)
                 nc.tensor.matmul_mx(
                     out=arg[:], lhsT=words.bitcast(FP4X4), lhsT_scale=scales,
-                    rhs=v_w[a][:].bitcast(FP8X4), rhs_scale=v_s[a][:], start=(a == 0), stop=(a == 1),
+                    rhs=v_w[a][:].bitcast(FP8X4), rhs_scale=v_s[:, a, :], start=(a == 0), stop=(a == 1),
                 )
             for a in range(2):
                 nc.tensor.matmul_mx(
                     out=lin[:], lhsT=w1_c[s, a].bitcast(FP8X4), lhsT_scale=w1_s[s, a],
-                    rhs=v_w[a][:].bitcast(FP8X4), rhs_scale=v_s[a][:], start=(a == 0), stop=(a == 1),
+                    rhs=v_w[a][:].bitcast(FP8X4), rhs_scale=v_s[:, a, :], start=(a == 0), stop=(a == 1),
                 )
-            mag = alloc(f"mag{s}", [PART, S], F32, tag=f"mag{s % 2}")
+            mag = alloc(f"mag{s}", [PART, S], F32, tag=mag_tags[s])
             cos = alloc(f"cos{s}", [PART, S], F32, tag=f"cos{s % 3}")
             nc.scalar.activation(mag[:], arg[:], ACT.Abs)
             nc.scalar.activation(cos[:], mag[:], ACT.Sin, bias=math.pi / 2, scale=-1.0)
@@ -229,22 +246,21 @@ def tile_list_powder_chip_binning_kernel(
             else:
                 weight = wgs_lo[:] if s < PACK else wgs_hi[:, s - PACK, :]
                 nc.vector.tensor_tensor(pages[s][:].indirect(lists[1][:]), put[s][:], weight, ALU.mult)
-            g1 = alloc(f"g1_{s}", [PART, P], F32, tag=g1_tags[s % 3] if s < SLICES - 1 else "lin_sb1")
-            g2 = alloc(f"g2_{s}", [PART, P], F32, tag=g2_tags[s % 3] if s < SLICES - 1 else "mag1")
+            g1 = alloc(f"g1_{s}", [PART, P], F32, tag=g1_tags[min(s, SLICES - 2) % 3])
+            g2 = alloc(f"g2_{s}", [PART, P], F32, tag=g2_tags[s % 3] if s != SLICES - 2 else "mag1")
             nc.vector.tensor_copy(g2[:], pages[s][:].indirect(lists[3][:]))
             nc.vector.tensor_copy(g1[:], pages[s][:].indirect(lists[2][:]))
             picked[s] = (g1, g2)
 
-        bias2 = [alloc(f"bias2_{b}", [PART, PACK], F32) for b in range(2)]
-        half_pw = alloc("half_pw", [PART, PACK], F32)
+        small = {}
 
         def finish(s, x1_out, x2_out):
             b, t = divmod(s, PACK)
             g1, g2 = picked[s]
-            eng = nc.gpsimd if USE_POOL else nc.vector
+            eng = nc.gpsimd if s < SLICES - 1 else nc.vector
             eng.tensor_scalar(x1_out, g1[:], F32_MAX, vec["low", b][:, t : t + 1], ALU.min, ALU.max)
             nc.scalar.activation(
-                x2_out, g2[:], ACT.Identity, bias=bias2[b][:, t : t + 1], scale=vec["gain", b][:, t : t + 1]
+                x2_out, g2[:], ACT.Identity, bias=small["bias", b][:, t : t + 1], scale=vec["gain", b][:, t : t + 1]
             )
 
         def quantise_x(name, grouped, tag):
@@ -253,7 +269,7 @@ def tile_list_powder_chip_binning_kernel(
             nc.vector.quantize_mx(
                 out=codes[:].bitcast(FP8X4), scales=scales[:], in_=grouped[:].rearrange("p m t -> p (m t)")
             )
-            return codes, scales
+            return codes[:], scales[:]
 
         e = [ps.tile([PART, P], F32, name=f"e{c}") for c in range(PACK)]
 
@@ -262,46 +278,55 @@ def tile_list_powder_chip_binning_kernel(
                 cols = slice(c * PART, (c + 1) * PART)
                 nc.tensor.matmul_mx(
                     out=e[c][:], lhsT=x1[0][:, cols].bitcast(FP8X4), lhsT_scale=x1[1][:, cols],
-                    rhs=x2[0][:].bitcast(FP8X4), rhs_scale=x2[1][:], start=(b == 0), stop=(b == 1),
+                    rhs=x2[0].bitcast(FP8X4), rhs_scale=x2[1], start=(b == 0), stop=(b == 1),
                 )
 
-        for b in range(2):
-            nc.gpsimd.tensor_tensor(bias2[b][:], vec["shift", b][:], vec["gain", b][:], ALU.mult)
-        nc.gpsimd.tensor_scalar(half_pw[:], pw_sb[:], 0.5, 0.0, ALU.mult, ALU.add)
+        def small_vectors():
+            cols = alloc("cols", [PART, 3, PACK], F32, tag="rows1")
+            for b in range(2):
+                small["bias", b] = cols[:, b, :]
+                nc.gpsimd.tensor_tensor(cols[:, b, :], vec["shift", b][:], vec["gain", b][:], ALU.mult)
+            small["half_pw"] = cols[:, 2, :]
+            nc.gpsimd.tensor_scalar(cols[:, 2, :], pw_sb[:], 0.5, 0.0, ALU.mult, ALU.add)
 
         planes = None
         flats = {}
         quantise_w1_lo(0)
         quantise_w1_lo(1)
-        for s in range(SLICES):
-            stage_one(s)
-            if s + 2 < PACK:
-                quantise_w1_lo(s + 2)
-            if s + 2 == PACK:
+        stage_one(0)
+        for s in range(SLICES - 1):
+            stage_one(s + 1)
+            if s == 0:
+                quantise_w1_lo(2)
+                small_vectors()
+            if s == 2:
                 quantise_w1_hi()
                 planes = alloc("planes", [PART, PACK, 2, P], BF16, tag="w1_raw_hi0")
-            if 2 <= s < PACK + 2:
+            if 1 <= s <= PACK:
+                r = s - 1
+                flats[r] = alloc(f"flat{r}", [PART, 2, P], BF16, tag=f"rows{r + 2}")
+                finish(r, flats[r][:, 0, :], flats[r][:, 1, :])
+            if 2 <= s <= PACK + 1:
                 r = s - 2
-                flat = alloc(f"flat{r}", [PART, 2, P], BF16, tag=f"rows{s}")
-                finish(r, flat[:, 0, :], flat[:, 1, :])
-                flats[r] = flat
-            if 3 <= s < PACK + 3:
-                r = s - 3
                 for t in range(PACK):
                     nc.sync.dma_start(out=planes[QUAD * r : QUAD * (r + 1), t, :, :], in_=flats[r][t:PART:PACK, :, :])
-            if s < SLICES - 1:
+            if s < SLICES - 2:
                 look_up(s)
 
-        lo = []
-        for i, (tag, ctag) in enumerate((("mag1", "put5"), ("lin_sb1", "put6"))):
-            grouped = alloc(f"x_lo{i}", [PART, P, PACK], BF16, tag=tag)
+        x_lo = alloc("x_lo", [PART, 2, P, PACK], BF16, tag="mag1")
+        for i in range(2):
             nc.scalar.copy(
-                out=grouped[:].rearrange("p (c i) t -> p c t i", i=4),
+                out=x_lo[:, i].rearrange("p (c i) t -> p c t i", i=4),
                 in_=planes[:, :, i, :].rearrange("p t (c i) -> p c t i", i=4),
             )
-            lo.append(quantise_x(f"x_lo{i}", grouped, ctag))
-        match(lo[0], lo[1], 0)
+        lo_c = alloc("x_lo_c", [PART, 2 * P], U32, tag="put5")
+        lo_s = alloc("x_lo_s", [PART, 2 * P], U8)
+        nc.vector.quantize_mx(
+            out=lo_c[:].bitcast(FP8X4), scales=lo_s[:], in_=x_lo[:].rearrange("p i m t -> p (i m t)")
+        )
+        match((lo_c[:, :P], lo_s[:, :P]), (lo_c[:, P:], lo_s[:, P:]), 0)
 
+        look_up(SLICES - 2)
         x1_hi = alloc("x1_hi", [PART, P, PACK], BF16, tag="rows7")
         x2_hi = alloc("x2_hi", [PART, P, PACK], BF16, tag="w1_raw_hi0")
         for s in range(PACK, SLICES - 1):
@@ -316,6 +341,6 @@ def tile_list_powder_chip_binning_kernel(
         for c in range(PACK):
             res = alloc(f"res{c}", [PART, P], F32, tag=f"put{c + 1}" if c < 3 else "put7")
             nc.scalar.activation(res[:], e[c][:], ACT.Tanh, scale=0.5)
-            col = half_pw[:, c : c + 1]
+            col = small["half_pw"][:, c : c + 1]
             nc.vector.tensor_scalar(res[:], res[:], col, col, ALU.mult, ALU.add)
             nc.sync.dma_start(out=out[c * PART : (c + 1) * PART, :], in_=res[:])

@@ -33,9 +33,18 @@ def tile_list_powder_chip_binning_kernel(
     nc = tc.nc
     with ExitStack() as ctx:
         sb = ctx.enter_context(tc.tile_pool(name="sb", bufs=1))
+        placed = ctx.enter_context(tc.tile_pool(name="placed", bufs=1))
         ps = ctx.enter_context(tc.psum_pool(name="ps", bufs=1))
+        row = 4 * S
+        at = {
+            "w1_g1_0": 0, "w1_g1_1": 2 * row - 2 * (row // 4), "put0": row,
+            "w1_gh": 4 * row, "g1_1": 4 * row,
+            "mag7": 8 * row, "x_lo": 8 * row, "g2_7": 8 * row, "g1_7": 9 * row,
+        }
 
         def alloc(name, shape, dtype, tag=None):
+            if name in at:
+                return placed.tile(shape, dtype, name=name, align_bytes=64, offset=at[name])
             return sb.tile(shape, dtype, name=name, tag=tag or name, align_bytes=64)
 
         lists = [alloc(f"list{i}", [PART, S // 16], U16) for i in range(4)]
@@ -43,9 +52,9 @@ def tile_list_powder_chip_binning_kernel(
         tab_s = alloc("tab_s", [PART, 2, T], U8)
         w4_w = alloc("w4_w", [PART, 2, 2 * H], U8)
         w4_s = [alloc(f"w4_s{b}", [PART, 2, PASS], U8) for b in range(2)]
-        groups = {0: 1, 1: 1, 2: 2}
+        groups = {0: 1, 1: 3}
         w1_raw = {
-            s: [alloc(f"w1_raw{s}_{a}", [PART, PACK, n * PART], F32) for a in range(2)] for s, n in ((0, 1), (1, 1), (2, 2))
+            s: [alloc(f"w1_raw{s}_{a}", [PART, PACK, n * PART], F32) for a in range(2)] for s, n in ((0, 1), (1, 3))
         }
         w1_raw_hi = [alloc(f"w1_raw_hi{a}", [PART, PACK, PASS], F32) for a in range(2)]
         rows = [alloc(f"rows{s}", [PART, S], F32) for s in range(SLICES)]
@@ -102,18 +111,17 @@ def tile_list_powder_chip_binning_kernel(
         load_table(0)
         load_w1_lo(0)
         load_table(1)
-        load_w1_lo(1)
         load_base(0)
+        load_w1_lo(1)
         nc.sync.dma_start(out=wgs_lo[:], in_=wgs)
         nc.sync.dma_start(lists[1][:], offs2)
         load_page(0)
         load_base(1)
         nc.sync.dma_start(lists[3][:], offs4)
         nc.sync.dma_start(lists[2][:], offs3)
-        load_w1_lo(2)
-        load_page(1)
         load_base(2)
         load_base(3)
+        load_page(1)
         for a in range(2):
             src = w1[a * PASS : (a + 1) * PASS, PASS:]
             nc.sync.dma_start(out=w1_raw_hi[a][:], in_=src.rearrange("(p j) c -> p j c", j=PACK))
@@ -154,26 +162,25 @@ def tile_list_powder_chip_binning_kernel(
 
         def quantise_w1_lo(s):
             width = groups[s] * PART
-            grouped = alloc(f"w1_g{s}", [PART, 2, width, PACK], BF16)
             for a in range(2):
-                copy = nc.vector.tensor_copy if s == 1 else nc.scalar.copy
+                grouped = alloc(f"w1_g{s}_{a}", [PART, width, PACK], BF16)
+                copy = nc.vector.tensor_copy if (s, a) == (1, 1) else nc.scalar.copy
                 copy(
-                    out=grouped[:, a].rearrange("p (c i) j -> p c j i", i=4),
+                    out=grouped[:].rearrange("p (c i) j -> p c j i", i=4),
                     in_=w1_raw[s][a][:].rearrange("p j (c i) -> p c j i", i=4),
                 )
-            codes = alloc(f"w1_c{s}", [PART, 2 * width], U32)
-            scales = alloc(f"w1_s{s}", [PART, 2 * width], U8)
-            nc.vector.quantize_mx(
-                out=codes[:].bitcast(FP8X4), scales=scales[:], in_=grouped[:].rearrange("p a c j -> p (a c j)")
-            )
-            for a in range(2):
+                codes = alloc(f"w1_c{s}_{a}", [PART, width], U32)
+                scales = alloc(f"w1_s{s}_{a}", [PART, width], U8)
+                nc.vector.quantize_mx(
+                    out=codes[:].bitcast(FP8X4), scales=scales[:], in_=grouped[:].rearrange("p c j -> p (c j)")
+                )
                 for u in range(groups[s]):
-                    cols = slice(a * width + u * PART, a * width + (u + 1) * PART)
+                    cols = slice(u * PART, (u + 1) * PART)
                     w1_c[s + u, a] = codes[:, cols]
                     w1_s[s + u, a] = scales[:, cols]
 
         def quantise_w1_hi():
-            grouped = alloc("w1_gh", [PART, 2, PACK, PART, PACK], BF16, tag="w1_raw2_1")
+            grouped = alloc("w1_gh", [PART, 2, PACK, PART, PACK], BF16)
             for a in range(2):
                 nc.scalar.copy(
                     out=grouped[:, a].rearrange("p t m j -> p m j t"),
@@ -195,10 +202,10 @@ def tile_list_powder_chip_binning_kernel(
                 return w4_w[:, a, 2 * PART * s : 2 * PART * (s + 1)], w4_s[0][:, a, PART * s : PART * (s + 1)]
             return w4_wd[:, a, s - PACK, :], w4_sd[:, a, s - PACK, :]
 
-        put_tags = ["w1_g1", "put1", "put2", "put3", "w1_g0", "put5", "put6", "put7"]
-        g1_tags = ["w1_g2", "g1_1", "g1_2"]
-        g2_tags = ["g2_0", "g2_1", "w1_raw2_1"]
-        mag_tags = ["mag0", "w1_g2", "mag0", "mag1", "w1_raw_hi1", "w1_raw_hi1", "mag0", "mag1"]
+        put_tags = [None, "put1", "put2", "put3", "put4", "put5", "put6", "put7"]
+        g1_tags = ["g1_a", "g1_b", "g1_c"]
+        g2_tags = ["g2_a", "g2_b", "g2_c"]
+        mag_tags = ["mag_a", "mag_b", "mag_a", "mag_b", "w1_raw_hi1", "w1_raw_hi1", "mag_a", None]
         put = {}
 
         def stage_one(s):
@@ -246,8 +253,8 @@ def tile_list_powder_chip_binning_kernel(
             else:
                 weight = wgs_lo[:] if s < PACK else wgs_hi[:, s - PACK, :]
                 nc.vector.tensor_tensor(pages[s][:].indirect(lists[1][:]), put[s][:], weight, ALU.mult)
-            g1 = alloc(f"g1_{s}", [PART, P], F32, tag=g1_tags[min(s, SLICES - 2) % 3])
-            g2 = alloc(f"g2_{s}", [PART, P], F32, tag=g2_tags[s % 3] if s != SLICES - 2 else "mag1")
+            g1 = alloc(f"g1_{s}", [PART, P], F32, tag=g1_tags[s % 3])
+            g2 = alloc(f"g2_{s}", [PART, P], F32, tag=g2_tags[s % 3])
             nc.vector.tensor_copy(g2[:], pages[s][:].indirect(lists[3][:]))
             nc.vector.tensor_copy(g1[:], pages[s][:].indirect(lists[2][:]))
             picked[s] = (g1, g2)
@@ -256,9 +263,12 @@ def tile_list_powder_chip_binning_kernel(
 
         def finish(s, x1_out, x2_out):
             b, t = divmod(s, PACK)
-            g1, g2 = picked[s]
-            eng = nc.gpsimd if s < SLICES - 1 else nc.vector
-            eng.tensor_scalar(x1_out, g1[:], F32_MAX, vec["low", b][:, t : t + 1], ALU.min, ALU.max)
+            nc.gpsimd.tensor_scalar(x1_out, picked[s][0][:], F32_MAX, vec["low", b][:, t : t + 1], ALU.min, ALU.max)
+            finish_x2(s, x2_out)
+
+        def finish_x2(s, x2_out):
+            b, t = divmod(s, PACK)
+            g2 = picked[s][1]
             nc.scalar.activation(
                 x2_out, g2[:], ACT.Identity, bias=small["bias", b][:, t : t + 1], scale=vec["gain", b][:, t : t + 1]
             )
@@ -297,9 +307,8 @@ def tile_list_powder_chip_binning_kernel(
         for s in range(SLICES - 1):
             stage_one(s + 1)
             if s == 0:
-                quantise_w1_lo(2)
                 small_vectors()
-            if s == 2:
+            if s == 1:
                 quantise_w1_hi()
                 planes = alloc("planes", [PART, PACK, 2, P], BF16, tag="w1_raw_hi0")
             if 1 <= s <= PACK:
@@ -313,18 +322,12 @@ def tile_list_powder_chip_binning_kernel(
             if s < SLICES - 2:
                 look_up(s)
 
-        x_lo = alloc("x_lo", [PART, 2, P, PACK], BF16, tag="mag1")
+        x_lo = alloc("x_lo", [PART, 2, P, PACK], BF16)
         for i in range(2):
             nc.scalar.copy(
                 out=x_lo[:, i].rearrange("p (c i) t -> p c t i", i=4),
                 in_=planes[:, :, i, :].rearrange("p t (c i) -> p c t i", i=4),
             )
-        lo_c = alloc("x_lo_c", [PART, 2 * P], U32, tag="put5")
-        lo_s = alloc("x_lo_s", [PART, 2 * P], U8)
-        nc.vector.quantize_mx(
-            out=lo_c[:].bitcast(FP8X4), scales=lo_s[:], in_=x_lo[:].rearrange("p i m t -> p (i m t)")
-        )
-        match((lo_c[:, :P], lo_s[:, :P]), (lo_c[:, P:], lo_s[:, P:]), 0)
 
         look_up(SLICES - 2)
         x1_hi = alloc("x1_hi", [PART, P, PACK], BF16, tag="rows7")
@@ -332,14 +335,32 @@ def tile_list_powder_chip_binning_kernel(
         for s in range(PACK, SLICES - 1):
             finish(s, x1_hi[:, :, s - PACK], x2_hi[:, :, s - PACK])
 
+        lo_c = alloc("x_lo_c", [PART, 2 * P], U32, tag="g1_a")
+        lo_s = alloc("x_lo_s", [PART, 2 * P], U8)
+        nc.vector.quantize_mx(
+            out=lo_c[:].bitcast(FP8X4), scales=lo_s[:], in_=x_lo[:].rearrange("p i m t -> p (i m t)")
+        )
+        match((lo_c[:, :P], lo_s[:, :P]), (lo_c[:, P:], lo_s[:, P:]), 0)
+
         look_up(SLICES - 1)
-        finish(SLICES - 1, x1_hi[:, :, PACK - 1], x2_hi[:, :, PACK - 1])
+        finish_x2(SLICES - 1, x2_hi[:, :, PACK - 1])
         x2q = quantise_x("x2_hi", x2_hi, "x2_hi_c")
-        x1q = quantise_x("x1_hi", x1_hi, "x1_hi_c")
-        match(x1q, x2q, 1)
+        x1_c = alloc("x1_hi_c", [PART, P], U32)
+        x1_s = alloc("x1_hi_s", [PART, P], U8)
+        for half in range(2):
+            cols = slice(half * P // 2, (half + 1) * P // 2)
+            nc.vector.tensor_scalar_max(
+                x1_hi[:, cols, PACK - 1], picked[SLICES - 1][0][:, cols], vec["low", 1][:, PACK - 1 : PACK]
+            )
+            nc.vector.quantize_mx(
+                out=x1_c[:, cols].bitcast(FP8X4),
+                scales=x1_s[:, cols],
+                in_=x1_hi[:, cols, :].rearrange("p m t -> p (m t)"),
+            )
+        match((x1_c[:], x1_s[:]), x2q, 1)
 
         for c in range(PACK):
-            res = alloc(f"res{c}", [PART, P], F32, tag=f"put{c + 1}" if c < 3 else "put7")
+            res = alloc(f"res{c}", [PART, P], F32, tag=("put2", "put5", "put6", "put7")[c])
             nc.scalar.activation(res[:], e[c][:], ACT.Tanh, scale=0.5)
             col = small["half_pw"][:, c : c + 1]
             nc.vector.tensor_scalar(res[:], res[:], col, col, ALU.mult, ALU.add)

@@ -38,7 +38,7 @@ def tile_list_powder_chip_binning_kernel(
         row = 4 * S
         at = {
             "w1_g1_0": 0, "w1_g1_1": 2 * row - 2 * (row // 4), "put0": row,
-            "w1_gh": 4 * row, "g1_1": 4 * row,
+            "w1_gh": 4 * row, "g2_2": 4 * row,
             "mag7": 8 * row, "x_lo": 8 * row, "g2_7": 8 * row, "g1_7": 9 * row,
         }
 
@@ -72,10 +72,9 @@ def tile_list_powder_chip_binning_kernel(
                 return mat[s * PART : (s + 1) * PART, :]
             return mat[PASS:, :].rearrange("(p t) c -> p t c", t=PACK)[:, s - PACK, :]
 
-        def load_w1_lo(s):
-            for a in range(2):
-                src = w1[a * PASS : (a + 1) * PASS, s * PART : (s + groups[s]) * PART]
-                nc.sync.dma_start(out=w1_raw[s][a][:], in_=src.rearrange("(p j) c -> p j c", j=PACK))
+        def load_w1_lo(s, a):
+            src = w1[a * PASS : (a + 1) * PASS, s * PART : (s + groups[s]) * PART]
+            nc.sync.dma_start(out=w1_raw[s][a][:], in_=src.rearrange("(p j) c -> p j c", j=PACK))
 
         def load_base(s):
             nc.sync.dma_start(out=rows[s][:], in_=slice_rows(base, s))
@@ -102,17 +101,19 @@ def tile_list_powder_chip_binning_kernel(
             )
 
         nc.sync.dma_start(lists[0][:], offs)
-        nc.sync.dma_start(out=w4_w[:].bitcast(I32), in_=w4_words.rearrange("a p c -> p a c").bitcast(I32))
+        load_table(0)
         for q in range(4):
             nc.sync.dma_start(
                 out=tab_s[QUAD * q : QUAD * q + 4, :, :].bitcast(I32),
                 in_=tab_scales[:, 4 * q : 4 * q + 4, :].rearrange("a r n -> r a n").bitcast(I32),
             )
-        load_table(0)
-        load_w1_lo(0)
         load_table(1)
+        nc.sync.dma_start(out=w4_w[:].bitcast(I32), in_=w4_words.rearrange("a p c -> p a c").bitcast(I32))
+        load_w1_lo(0, 0)
+        load_w1_lo(0, 1)
+        load_w1_lo(1, 0)
         load_base(0)
-        load_w1_lo(1)
+        load_w1_lo(1, 1)
         nc.sync.dma_start(out=wgs_lo[:], in_=wgs)
         nc.sync.dma_start(lists[1][:], offs2)
         load_page(0)
@@ -344,7 +345,6 @@ def tile_list_powder_chip_binning_kernel(
 
         look_up(SLICES - 1)
         finish_x2(SLICES - 1, x2_hi[:, :, PACK - 1])
-        x2q = quantise_x("x2_hi", x2_hi, "x2_hi_c")
         x1_c = alloc("x1_hi_c", [PART, P], U32)
         x1_s = alloc("x1_hi_s", [PART, P], U8)
         for half in range(2):
@@ -352,6 +352,8 @@ def tile_list_powder_chip_binning_kernel(
             nc.vector.tensor_scalar_max(
                 x1_hi[:, cols, PACK - 1], picked[SLICES - 1][0][:, cols], vec["low", 1][:, PACK - 1 : PACK]
             )
+            if half == 0:
+                x2q = quantise_x("x2_hi", x2_hi, "x2_hi_c")
             nc.vector.quantize_mx(
                 out=x1_c[:, cols].bitcast(FP8X4),
                 scales=x1_s[:, cols],

import math
from contextlib import ExitStack

import concourse.mybir as mybir

K, H, T, S, T2, P = 1024, 1024, 2048, 512, 1024, 512
FLOPS = 2 * K * H * S * 2 + 2 * H * P * P

F32 = mybir.dt.float32
BF16 = mybir.dt.bfloat16
I32 = mybir.dt.int32
U32 = mybir.dt.uint32
U16 = mybir.dt.uint16
U8 = mybir.dt.uint8
FP8X4 = mybir.dt.float8_e4m3fn_x4
FP4X4 = mybir.dt.float4_e2m1fn_x4
ALU = mybir.AluOpType
ACT = mybir.ActivationFunctionType

PART = 128
PACK = 4
PASS = PART * PACK
QUAD = 32
SLICES = H // PART
F32_MAX = 3.4028234663852886e38
USE_POOL = True


def tile_list_powder_chip_binning_kernel(
    tc, tab_words, tab_scales, w1, w4_words, w4_scales, base, wgs, page0, low, shift, gain, pw,
    offs, offs2, offs3, offs4, out,
):
    nc = tc.nc
    with ExitStack() as ctx:
        sb = ctx.enter_context(tc.tile_pool(name="sb", bufs=1))
        placed = ctx.enter_context(tc.tile_pool(name="placed", bufs=1))
        ps = ctx.enter_context(tc.psum_pool(name="ps", bufs=1))
        row = 4 * S
        at = {
            "w1_g1_0": 0, "w1_g1_1": 2 * row - 2 * (row // 4), "put0": row,
            "w1_gh": 4 * row, "g2_2": 4 * row,
            "mag7": 8 * row, "x_lo": 8 * row, "g2_7": 8 * row, "g1_7": 9 * row,
        }

        def alloc(name, shape, dtype, tag=None):
            if name in at:
                return placed.tile(shape, dtype, name=name, align_bytes=64, offset=at[name])
            return sb.tile(shape, dtype, name=name, tag=tag or name, align_bytes=64)

        lists = [alloc(f"list{i}", [PART, S // 16], U16) for i in range(4)]
        tab_w = [alloc(f"tab_w{a}", [PART, T], U32) for a in range(2)]
        tab_s = alloc("tab_s", [PART, 2, T], U8)
        w4_w = alloc("w4_w", [PART, 2, 2 * H], U8)
        w4_s = [alloc(f"w4_s{b}", [PART, 2, PASS], U8) for b in range(2)]
        groups = {0: 1, 1: 3}
        w1_raw = {
            s: [alloc(f"w1_raw{s}_{a}", [PART, PACK, n * PART], F32) for a in range(2)] for s, n in ((0, 1), (1, 3))
        }
        w1_raw_hi = [alloc(f"w1_raw_hi{a}", [PART, PACK, PASS], F32) for a in range(2)]
        rows = [alloc(f"rows{s}", [PART, S], F32) for s in range(SLICES)]
        pages = [alloc(f"page{s}", [PART, T2], F32) for s in range(SLICES)]
        wgs_lo = alloc("wgs_lo", [PART, S], F32)
        wgs_hi = alloc("wgs_hi", [PART, PACK, S], F32)
        vec = {}
        for name in ("low", "shift", "gain"):
            for b in range(2):
                vec[name, b] = alloc(f"{name}{b}", [PART, PACK], F32)
        pw_sb = alloc("pw_sb", [PART, PACK], F32)

        def slice_rows(mat, s):
            if s < PACK:
                return mat[s * PART : (s + 1) * PART, :]
            return mat[PASS:, :].rearrange("(p t) c -> p t c", t=PACK)[:, s - PACK, :]

        def load_w1_lo(s, a):
            src = w1[a * PASS : (a + 1) * PASS, s * PART : (s + groups[s]) * PART]
            nc.sync.dma_start(out=w1_raw[s][a][:], in_=src.rearrange("(p j) c -> p j c", j=PACK))

        def load_base(s):
            nc.sync.dma_start(out=rows[s][:], in_=slice_rows(base, s))

        def load_page(s):
            nc.sync.dma_start(out=pages[s][:], in_=slice_rows(page0, s))

        warm = alloc("warm", [PART, 2], F32)
        nc.vector.memset(warm[:, 0:1], 0.0)
        nc.scalar.activation(warm[:, 1:2], warm[:, 0:1], ACT.Silu)
        nc.vector.memset(tab_s[:].rearrange("p a n -> p (a n)").bitcast(I32), 0)
        nc.vector.memset(w4_s[1][:].rearrange("p a n -> p (a n)").bitcast(I32), 0)
        for b, queue in ((0, nc.scalar), (1, nc.gpsimd)):
            for q in range(4):
                src = w4_scales[:, 4 * q : 4 * q + 4, b * PASS : (b + 1) * PASS]
                queue.dma_start(
                    out=w4_s[b][QUAD * q : QUAD * q + 4, :, :].bitcast(I32),
                    in_=src.rearrange("a r n -> r a n").bitcast(I32),
                )

        def load_table(a):
            nc.sync.dma_start(
                out=tab_w[a][:].bitcast(I32), in_=tab_words[a].rearrange("p n t -> p (n t)").bitcast(I32)
            )

        nc.sync.dma_start(lists[0][:], offs)
        load_table(0)
        for q in range(4):
            nc.sync.dma_start(
                out=tab_s[QUAD * q : QUAD * q + 4, :, :].bitcast(I32),
                in_=tab_scales[:, 4 * q : 4 * q + 4, :].rearrange("a r n -> r a n").bitcast(I32),
            )
        load_table(1)
        nc.sync.dma_start(out=w4_w[:].bitcast(I32), in_=w4_words.rearrange("a p c -> p a c").bitcast(I32))
        load_w1_lo(0, 0)
        load_w1_lo(0, 1)
        load_w1_lo(1, 0)
        load_base(0)
        load_w1_lo(1, 1)
        nc.sync.dma_start(out=wgs_lo[:], in_=wgs)
        nc.sync.dma_start(lists[1][:], offs2)
        load_page(0)
        load_base(1)
        nc.sync.dma_start(lists[3][:], offs4)
        nc.sync.dma_start(lists[2][:], offs3)
        load_base(2)
        load_base(3)
        load_page(1)
        for a in range(2):
            src = w1[a * PASS : (a + 1) * PASS, PASS:]
            nc.sync.dma_start(out=w1_raw_hi[a][:], in_=src.rearrange("(p j) c -> p j c", j=PACK))
        load_page(2)
        with nc.allow_non_contiguous_dma(reason="one value to a partition"):
            for name, src in (("low", low), ("shift", shift), ("gain", gain)):
                nc.sync.dma_start(out=vec[name, 0][:], in_=src[:PASS].rearrange("(s p) -> p s", p=PART))
                nc.sync.dma_start(out=vec[name, 1][:], in_=src[PASS:].rearrange("(p t) -> p t", t=PACK))
            nc.sync.dma_start(out=pw_sb[:], in_=pw.rearrange("(c p) -> p c", p=PART))
        load_page(3)
        load_base(4)
        for q in range(4):
            nc.sync.dma_start(
                out=wgs_hi[QUAD * q : QUAD * (q + 1), :, :], in_=wgs.rearrange("(p t) j -> p t j", t=PACK)
            )
        for s in range(PACK + 1, SLICES):
            load_base(s)
        for s in range(PACK, SLICES):
            load_page(s)

        v_w = [alloc(f"v_w{a}", [PART, S], U32) for a in range(2)]
        for a in range(2):
            nc.vector.tensor_copy(v_w[a][:], tab_w[a][:].indirect(lists[0][:]))
        v_s = alloc("v_s", [PART, 2, S], U8)
        for a in range(2):
            nc.vector.tensor_copy(v_s[:, a, :], tab_s[:, a, :].indirect(lists[0][:]))

        w4_wd = alloc("w4_wd", [PART, 2, PACK, 2 * PART], U8)
        w4_sd = alloc("w4_sd", [PART, 2, PACK, PART], U8)
        nc.vector.tensor_copy(
            out=w4_wd[:].bitcast(U16),
            in_=w4_w[:].bitcast(U16)[:, :, PASS:].rearrange("p a (m t) -> p a t m", t=PACK),
        )
        nc.gpsimd.tensor_copy(out=w4_sd[:], in_=w4_s[1][:].rearrange("p a (m t) -> p a t m", t=PACK))

        w1_c = {}
        w1_s = {}

        def quantise_w1_lo(s):
            width = groups[s] * PART
            for a in range(2):
                grouped = alloc(f"w1_g{s}_{a}", [PART, width, PACK], BF16)
                copy = nc.vector.tensor_copy if (s, a) == (1, 1) else nc.scalar.copy
                copy(
                    out=grouped[:].rearrange("p (c i) j -> p c j i", i=4),
                    in_=w1_raw[s][a][:].rearrange("p j (c i) -> p c j i", i=4),
                )
                codes = alloc(f"w1_c{s}_{a}", [PART, width], U32)
                scales = alloc(f"w1_s{s}_{a}", [PART, width], U8)
                nc.vector.quantize_mx(
                    out=codes[:].bitcast(FP8X4), scales=scales[:], in_=grouped[:].rearrange("p c j -> p (c j)")
                )
                for u in range(groups[s]):
                    cols = slice(u * PART, (u + 1) * PART)
                    w1_c[s + u, a] = codes[:, cols]
                    w1_s[s + u, a] = scales[:, cols]

        def quantise_w1_hi():
            grouped = alloc("w1_gh", [PART, 2, PACK, PART, PACK], BF16)
            for a in range(2):
                nc.scalar.copy(
                    out=grouped[:, a].rearrange("p t m j -> p m j t"),
                    in_=w1_raw_hi[a][:].rearrange("p j (m t) -> p m j t", t=PACK),
                )
            codes = alloc("w1_ch", [PART, 2 * PASS], U32)
            scales = alloc("w1_sh", [PART, 2 * PASS], U8)
            nc.vector.quantize_mx(
                out=codes[:].bitcast(FP8X4), scales=scales[:], in_=grouped[:].rearrange("p a t m j -> p (a t m j)")
            )
            for a in range(2):
                for t in range(PACK):
                    cols = slice(a * PASS + t * PART, a * PASS + (t + 1) * PART)
                    w1_c[PACK + t, a] = codes[:, cols]
                    w1_s[PACK + t, a] = scales[:, cols]

        def w4_operand(s, a):
            if s < PACK:
                return w4_w[:, a, 2 * PART * s : 2 * PART * (s + 1)], w4_s[0][:, a, PART * s : PART * (s + 1)]
            return w4_wd[:, a, s - PACK, :], w4_sd[:, a, s - PACK, :]

        put_tags = [None, "put1", "put2", "put3", "put4", "put5", "put6", "put7"]
        g1_tags = ["g1_a", "g1_b", "g1_c"]
        g2_tags = ["g2_a", "g2_b", "g2_c"]
        mag_tags = ["mag_a", "mag_b", "mag_a", "mag_b", "w1_raw_hi1", "w1_raw_hi1", "mag_a", None]
        put = {}

        def stage_one(s):
            arg = ps.tile([PART, S], F32, name=f"arg{s}", tag=f"arg{s % 2}")
            lin = ps.tile([PART, S], F32, name=f"lin{s}", tag=f"lin{s % 2}")
            for a in range(2):
                words, scales = w4_operand(s, a)
                nc.tensor.matmul_mx(
                    out=arg[:], lhsT=words.bitcast(FP4X4), lhsT_scale=scales,
                    rhs=v_w[a][:].bitcast(FP8X4), rhs_scale=v_s[:, a, :], start=(a == 0), stop=(a == 1),
                )
            for a in range(2):
                nc.tensor.matmul_mx(
                    out=lin[:], lhsT=w1_c[s, a].bitcast(FP8X4), lhsT_scale=w1_s[s, a],
                    rhs=v_w[a][:].bitcast(FP8X4), rhs_scale=v_s[:, a, :], start=(a == 0), stop=(a == 1),
                )
            mag = alloc(f"mag{s}", [PART, S], F32, tag=mag_tags[s])
            cos = alloc(f"cos{s}", [PART, S], F32, tag=f"cos{s % 3}")
            nc.scalar.activation(mag[:], arg[:], ACT.Abs)
            nc.scalar.activation(cos[:], mag[:], ACT.Sin, bias=math.pi / 2, scale=-1.0)
            weight = wgs_lo[:] if s < PACK else wgs_hi[:, s - PACK, :]
            h = rows[s]
            if not USE_POOL:
                put[s] = alloc(f"put{s}", [PART, S], F32, tag=put_tags[s])
                nc.vector.tensor_tensor(h[:], lin[:], h[:], ALU.add)
                nc.vector.tensor_tensor(put[s][:], h[:], cos[:], ALU.mult)
                return
            if s == 0:
                eng = nc.vector
                eng.tensor_tensor(h[:], lin[:], h[:], ALU.add)
            else:
                eng = nc.gpsimd
                lin_sb = alloc(f"lin_sb{s}", [PART, S], F32, tag=f"lin_sb{s % 3}")
                nc.scalar.copy(out=lin_sb[:], in_=lin[:])
                eng.tensor_tensor(h[:], lin_sb[:], h[:], ALU.add)
            eng.tensor_tensor(h[:], h[:], cos[:], ALU.mult)
            put[s] = alloc(f"put{s}", [PART, S], F32, tag=put_tags[s])
            eng.tensor_tensor(put[s][:], h[:], weight, ALU.mult)

        picked = {}

        def look_up(s):
            if USE_POOL:
                nc.vector.tensor_copy(pages[s][:].indirect(lists[1][:]), put[s][:])
            else:
                weight = wgs_lo[:] if s < PACK else wgs_hi[:, s - PACK, :]
                nc.vector.tensor_tensor(pages[s][:].indirect(lists[1][:]), put[s][:], weight, ALU.mult)
            g1 = alloc(f"g1_{s}", [PART, P], F32, tag=g1_tags[s % 3])
            g2 = alloc(f"g2_{s}", [PART, P], F32, tag=g2_tags[s % 3])
            nc.vector.tensor_copy(g2[:], pages[s][:].indirect(lists[3][:]))
            nc.vector.tensor_copy(g1[:], pages[s][:].indirect(lists[2][:]))
            picked[s] = (g1, g2)

        small = {}

        def finish(s, x1_out, x2_out):
            b, t = divmod(s, PACK)
            nc.gpsimd.tensor_scalar(x1_out, picked[s][0][:], F32_MAX, vec["low", b][:, t : t + 1], ALU.min, ALU.max)
            finish_x2(s, x2_out)

        def finish_x2(s, x2_out):
            b, t = divmod(s, PACK)
            g2 = picked[s][1]
            nc.scalar.activation(
                x2_out, g2[:], ACT.Identity, bias=small["bias", b][:, t : t + 1], scale=vec["gain", b][:, t : t + 1]
            )

        def quantise_x(name, grouped, tag):
            codes = alloc(f"{name}_c", [PART, P], U32, tag=tag)
            scales = alloc(f"{name}_s", [PART, P], U8)
            nc.vector.quantize_mx(
                out=codes[:].bitcast(FP8X4), scales=scales[:], in_=grouped[:].rearrange("p m t -> p (m t)")
            )
            return codes[:], scales[:]

        e = [ps.tile([PART, P], F32, name=f"e{c}") for c in range(PACK)]

        def match(x1, x2, b):
            for c in range(PACK):
                cols = slice(c * PART, (c + 1) * PART)
                nc.tensor.matmul_mx(
                    out=e[c][:], lhsT=x1[0][:, cols].bitcast(FP8X4), lhsT_scale=x1[1][:, cols],
                    rhs=x2[0].bitcast(FP8X4), rhs_scale=x2[1], start=(b == 0), stop=(b == 1),
                )

        def small_vectors():
            cols = alloc("cols", [PART, 3, PACK], F32, tag="rows1")
            for b in range(2):
                small["bias", b] = cols[:, b, :]
                nc.gpsimd.tensor_tensor(cols[:, b, :], vec["shift", b][:], vec["gain", b][:], ALU.mult)
            small["half_pw"] = cols[:, 2, :]
            nc.gpsimd.tensor_scalar(cols[:, 2, :], pw_sb[:], 0.5, 0.0, ALU.mult, ALU.add)

        planes = None
        flats = {}
        quantise_w1_lo(0)
        quantise_w1_lo(1)
        stage_one(0)
        for s in range(SLICES - 1):
            stage_one(s + 1)
            if s == 0:
                small_vectors()
            if s == 1:
                quantise_w1_hi()
                planes = alloc("planes", [PART, PACK, 2, P], BF16, tag="w1_raw_hi0")
            if 1 <= s <= PACK:
                r = s - 1
                flats[r] = alloc(f"flat{r}", [PART, 2, P], BF16, tag=f"rows{r + 2}")
                finish(r, flats[r][:, 0, :], flats[r][:, 1, :])
            if 2 <= s <= PACK + 1:
                r = s - 2
                for t in range(PACK):
                    nc.sync.dma_start(out=planes[QUAD * r : QUAD * (r + 1), t, :, :], in_=flats[r][t:PART:PACK, :, :])
            if s < SLICES - 2:
                look_up(s)

        x_lo = alloc("x_lo", [PART, 2, P, PACK], BF16)
        for i in range(2):
            nc.scalar.copy(
                out=x_lo[:, i].rearrange("p (c i) t -> p c t i", i=4),
                in_=planes[:, :, i, :].rearrange("p t (c i) -> p c t i", i=4),
            )

        look_up(SLICES - 2)
        x1_hi = alloc("x1_hi", [PART, P, PACK], BF16, tag="rows7")
        x2_hi = alloc("x2_hi", [PART, P, PACK], BF16, tag="w1_raw_hi0")
        for s in range(PACK, SLICES - 1):
            finish(s, x1_hi[:, :, s - PACK], x2_hi[:, :, s - PACK])

        lo_c = alloc("x_lo_c", [PART, 2 * P], U32, tag="g1_a")
        lo_s = alloc("x_lo_s", [PART, 2 * P], U8)
        nc.vector.quantize_mx(
            out=lo_c[:].bitcast(FP8X4), scales=lo_s[:], in_=x_lo[:].rearrange("p i m t -> p (i m t)")
        )
        match((lo_c[:, :P], lo_s[:, :P]), (lo_c[:, P:], lo_s[:, P:]), 0)

        look_up(SLICES - 1)
        finish_x2(SLICES - 1, x2_hi[:, :, PACK - 1])
        x1_c = alloc("x1_hi_c", [PART, P], U32)
        x1_s = alloc("x1_hi_s", [PART, P], U8)
        for half in range(2):
            cols = slice(half * P // 2, (half + 1) * P // 2)
            nc.vector.tensor_scalar_max(
                x1_hi[:, cols, PACK - 1], picked[SLICES - 1][0][:, cols], vec["low", 1][:, PACK - 1 : PACK]
            )
            if half == 0:
                x2q = quantise_x("x2_hi", x2_hi, "x2_hi_c")
            nc.vector.quantize_mx(
                out=x1_c[:, cols].bitcast(FP8X4),
                scales=x1_s[:, cols],
                in_=x1_hi[:, cols, :].rearrange("p m t -> p (m t)"),
            )
        match((x1_c[:], x1_s[:]), x2q, 1)

        for c in range(PACK):
            res = alloc(f"res{c}", [PART, P], F32, tag=("put2", "put5", "put6", "put7")[c])
            nc.scalar.activation(res[:], e[c][:], ACT.Tanh, scale=0.5)
            col = small["half_pw"][:, c : c + 1]
            nc.vector.tensor_scalar(res[:], res[:], col, col, ALU.mult, ALU.add)
            nc.sync.dma_start(out=out[c * PART : (c + 1) * PART, :], in_=res[:])
